import numpy as np
import ml_dtypes


def mxq(x, axis, fmt="e4m3"):
    dtype, down = {"e4m3": (ml_dtypes.float8_e4m3fn, 7), "e5m2": (ml_dtypes.float8_e5m2, 14)}[fmt]
    v = np.moveaxis(np.asarray(x, np.float32).astype(ml_dtypes.bfloat16).astype(np.float64), axis, -1)
    blocks = v.reshape(v.shape[:-1] + (-1, 32))
    amax = np.abs(blocks).max(-1, keepdims=True)
    byte = np.maximum(np.where(amax > 0, np.frexp(amax)[1] - 1 + 127, 0) - down, 1)
    scale = np.exp2(byte - 127.0)
    codes = (blocks / scale).astype(np.float32).astype(dtype).astype(np.float64)
    return np.moveaxis((codes * scale).reshape(v.shape), -1, axis)


WIDE = False


def mx_kscale(k):
    if not WIDE:
        return np.ones(k)
    levels = np.array([10, -10, 5, -5, 0])
    if k % 512:
        return np.exp2(np.random.permutation(np.resize(levels, k // 32))).repeat(32)
    a = np.empty((k // 512, 16))
    for p in range(k // 512):
        a[p, :8] = np.random.permutation(np.resize(levels, 8))
        for g in range(8):
            far = levels[np.abs(levels - a[p, g]) >= 10]
            a[p, g + 8] = far[np.random.randint(len(far))]
    return np.exp2(a.ravel()).repeat(32)


def f64(x):
    return np.asarray(x).astype(np.float64)


def striped(idx):
    return np.tile(idx.reshape(-1, 16).T, (8, 1)).astype(np.uint16)


def unstriped(offs):
    return offs[:16].T.reshape(-1).astype(np.int64)


def gelu(v):
    return 0.5 * v * (1.0 + np.tanh(np.sqrt(2.0 / np.pi) * (v + 0.044715 * v**3)))


K, T, D, S, V, H, N = 512, 1024, 4, 1024, 256, 1024, 256


def setup_inputs():
    n = np.random.standard_normal
    s = mx_kscale(K)[:, None]
    u = mx_kscale(H)
    return {
        "xT": (n((K, T)) * s).astype(np.float32),
        "w1": (n((K, H)) / np.sqrt(K) / s * u).astype(np.float32),
        "w2": (n((H, N)) / np.sqrt(H) / u[:, None]).astype(np.float32),
        "offs": striped(np.concatenate([np.random.permutation(T)[:V] for _ in range(D)])),
    }


def reference(xT, w1, w2, offs):
    idx = unstriped(offs)
    x = np.empty((K, V))
    for l in range(D):
        r = l // 4 * (4 * K // D) + l % 4 + 4 * np.arange(K // D)
        x[r] = f64(xT)[r][:, idx[l * V:(l + 1) * V]]
    xq = mxq(x, 0, "e4m3")
    h = gelu(mxq(f64(w1), 0, "e4m3").T @ xq)
    return mxq(f64(w2), 0, "e4m3").T @ mxq(h, 0, "e4m3")

@@ -1,0 +1,141 @@
+from contextlib import ExitStack
+
+import concourse.mybir as mybir
+
+F32 = mybir.dt.float32
+BF16 = mybir.dt.bfloat16
+U32 = mybir.dt.uint32
+U16 = mybir.dt.uint16
+U8 = mybir.dt.uint8
+FP8X4 = mybir.dt.float8_e4m3fn_x4
+GELU = mybir.ActivationFunctionType.Gelu_apprx_tanh
+P = 128
+K, T, H, N, V, L = 512, 1024, 1024, 256, 256, 4
+FLOPS = 2 * V * (K * H + H * N)
+
+
+def tile_picked_grid_mlp_gelu_sub_l_kernel(tc, xT, w1, w2, offs, out):
+    nc = tc.nc
+    with ExitStack() as ctx:
+        held = ctx.enter_context(tc.tile_pool(name="held", bufs=1))
+        psum = ctx.enter_context(tc.psum_pool(name="psum", bufs=1))
+
+        offsets = held.tile([P, L * V // 16], U16, name="offsets")
+        level = [held.tile([P, T], F32, name="level%d" % l) for l in range(L)]
+        w1a_raw = held.tile([P, 4, 512], F32, name="w1a_raw")
+        w1b_raw = [held.tile([P, 2, 512], F32, name="w1b_raw%d" % i) for i in range(2)]
+        w2_raw = [held.tile([P, 4, N], F32, name="w2_raw%d" % g) for g in range(2)]
+
+        x_bf = held.tile([P, V, 4], BF16, name="x_bf", align_bytes=64)
+        x_codes = held.tile([P, V], U32, name="x_codes", align_bytes=64)
+        x_scales = held.tile([P, V], U8, name="x_scales", align_bytes=64)
+        w1_store = [held.tile([P, 1024], U32, name="w1_store%d" % g, align_bytes=64) for g in range(2)]
+        w1_bf = [w1_store[g][:].bitcast(BF16) for g in range(2)]
+        w1_codes = [held.tile([P, 512], U32, name="w1_codes%d" % g, align_bytes=64) for g in range(2)]
+        w1_scales = [held.tile([P, 512], U8, name="w1_scales%d" % g, align_bytes=64) for g in range(2)]
+        w2_codes = [held.tile([P, N], U32, name="w2_codes%d" % g, align_bytes=64) for g in range(2)]
+        w2_scales = [held.tile([P, N], U8, name="w2_scales%d" % g, align_bytes=64) for g in range(2)]
+        h_bf = [[held.tile([P, P, 4], BF16, name="h_bf%d%d" % (g, n), align_bytes=64) for n in range(2)] for g in range(2)]
+        h_own = [held.tile([P, P], U32, name="h_codes%d" % n, align_bytes=64) for n in range(2)]
+        h_codes = [[x_codes[:, P * n : P * n + P] for n in range(2)], [h_own[n][:] for n in range(2)]]
+        h_own_scales = [held.tile([P, P], U8, name="h_scales%d" % n, align_bytes=64) for n in range(2)]
+        h_scales = [[x_scales[:, P * n : P * n + P] for n in range(2)], [h_own_scales[n][:] for n in range(2)]]
+        out_sb = [[held.tile([P, P], F32, name="out_sb%d%d" % (m, n)) for n in range(2)] for m in range(2)]
+        h_ps = [[psum.tile([P, 4, P], F32, name="h_ps%d%d" % (g, n)) for n in range(2)] for g in range(2)]
+        out_ps = [[psum.tile([P, 512], F32, name="out_ps%d%d" % (m, n)) for n in range(2)] for m in range(2)]
+        warm = held.tile([P, 2], F32, name="warm")
+
+        w1_rows = w1.rearrange("(p j) c -> p j c", j=4)
+        w2_rows = w2.rearrange("(g p j) c -> g p j c", g=2, j=4)
+        x_rows = xT.rearrange("(p l) c -> l p c", l=4)
+
+        nc.sync.dma_start(offsets[:], offs)
+        nc.sync.dma_start(w1a_raw[:], w1_rows[:, :, 0:512])
+        for l in range(L):
+            nc.sync.dma_start(level[l][:], x_rows[l])
+        for i in range(2):
+            nc.sync.dma_start(w1b_raw[i][:], w1_rows[:, 2 * i : 2 * i + 2, 512:1024])
+        for g in range(2):
+            nc.sync.dma_start(w2_raw[g][:], w2_rows[g])
+
+        nc.vector.memset(warm[:], 0.0)
+        nc.scalar.activation(warm[:, 1:2], warm[:, 0:1], GELU)
+
+        def cast_w1(copy, g, j0, raw, lo, hi):
+            copy(
+                w1_bf[g].rearrange("p (t m j) -> p m t j", t=4, j=4)[:, lo:hi, :, j0 : j0 + raw.shape[1]],
+                raw[:].rearrange("p j (m t) -> p m t j", t=4)[:, lo:hi],
+            )
+
+        def quantise_w1(g, half):
+            w = slice(256 * half, 256 * half + 256)
+            nc.vector.quantize_mx(
+                out=w1_codes[g][:, w].bitcast(FP8X4),
+                scales=w1_scales[g][:, w],
+                in_=w1_bf[g][:, 1024 * half : 1024 * half + 1024],
+            )
+
+        def prepare_w2(g):
+            grouped = w1_bf[1 - g][:, 0:1024]
+            nc.vector.tensor_copy(grouped.rearrange("p (c j) -> p c j", j=4), w2_raw[g][:].rearrange("p j c -> p c j"))
+            nc.vector.quantize_mx(out=w2_codes[g][:].bitcast(FP8X4), scales=w2_scales[g][:], in_=grouped)
+
+        def quantise(codes, scales, src):
+            nc.vector.quantize_mx(out=codes.bitcast(FP8X4), scales=scales, in_=src[:].rearrange("p n j -> p (n j)"))
+
+        def layer1(g, n):
+            v = slice(P * n, P * n + P)
+            for t in range(4):
+                m = slice(P * t, P * t + P)
+                nc.tensor.matmul_mx(
+                    out=h_ps[g][n][:, t, :],
+                    lhsT=w1_codes[g][:, m].bitcast(FP8X4),
+                    lhsT_scale=w1_scales[g][:, m],
+                    rhs=x_codes[:, v].bitcast(FP8X4),
+                    rhs_scale=x_scales[:, v],
+                    start=True,
+                    stop=True,
+                )
+            nc.scalar.activation(h_bf[g][n][:], h_ps[g][n][:].rearrange("p t n -> p n t"), GELU)
+
+        def layer2(g, n):
+            for mt in range(2):
+                m = slice(P * mt, P * mt + P)
+                nc.tensor.matmul_mx(
+                    out=out_ps[mt][n][:, 0:P],
+                    lhsT=w2_codes[g][:, m].bitcast(FP8X4),
+                    lhsT_scale=w2_scales[g][:, m],
+                    rhs=h_codes[g][n].bitcast(FP8X4),
+                    rhs_scale=h_scales[g][n],
+                    start=(g == 0),
+                    stop=(g == 1),
+                )
+
+        cast_w1(nc.vector.tensor_copy, 0, 0, w1a_raw, 0, 72)
+        cast_w1(nc.scalar.copy, 0, 0, w1a_raw, 72, 128)
+        for half in range(2):
+            quantise_w1(0, half)
+        for l in range(L):
+            nc.vector.tensor_copy(x_bf[:, :, l], level[l][:].indirect(offsets[:, 16 * l : 16 * l + 16]))
+        quantise(x_codes[:], x_scales[:], x_bf)
+        for n in range(2):
+            layer1(0, n)
+        for i in range(2):
+            cast_w1(nc.vector.tensor_copy, 1, 2 * i, w1b_raw[i], 0, 128)
+        for half in range(2):
+            quantise_w1(1, half)
+        for n in range(2):
+            layer1(1, n)
+        for n in range(2):
+            quantise(h_codes[0][n], h_scales[0][n], h_bf[0][n])
+        for g in range(2):
+            prepare_w2(g)
+        for n in range(2):
+            layer2(0, n)
+        for n in range(2):
+            quantise(h_codes[1][n], h_scales[1][n], h_bf[1][n])
+            layer2(1, n)
+            nc.vector.tensor_copy(out_sb[0][n][:], out_ps[0][n][:, 0:P])
+            nc.scalar.copy(out_sb[1][n][:], out_ps[1][n][:, 0:P])
+            nc.sync.dma_start(out[0:P, P * n : P * n + P], out_sb[0][n][:])
+            nc.scalar.dma_start(out[P : 2 * P, P * n : P * n + P], out_sb[1][n][:])

@@ -20,39 +20,51 @@ def tile_picked_grid_mlp_gelu_sub_l_kernel(tc, xT, w1, w2, offs, out):
         held = ctx.enter_context(tc.tile_pool(name="held", bufs=1))
         psum = ctx.enter_context(tc.psum_pool(name="psum", bufs=1))
 
-        offsets = held.tile([P, L * V // 16], U16, name="offsets")
-        level = [held.tile([P, T], F32, name="level%d" % l) for l in range(L)]
-        w1a_raw = held.tile([P, 4, 512], F32, name="w1a_raw")
-        w1b_raw = [held.tile([P, 2, 512], F32, name="w1b_raw%d" % i) for i in range(2)]
-        w2_raw = [held.tile([P, 4, N], F32, name="w2_raw%d" % g) for g in range(2)]
+        def sb(shape, dtype, name):
+            return held.tile(shape, dtype, name=name, align_bytes=64)
 
-        x_bf = held.tile([P, V, 4], BF16, name="x_bf", align_bytes=64)
-        x_codes = held.tile([P, V], U32, name="x_codes", align_bytes=64)
-        x_scales = held.tile([P, V], U8, name="x_scales", align_bytes=64)
-        w1_store = [held.tile([P, 1024], U32, name="w1_store%d" % g, align_bytes=64) for g in range(2)]
-        w1_bf = [w1_store[g][:].bitcast(BF16) for g in range(2)]
-        w1_codes = [held.tile([P, 512], U32, name="w1_codes%d" % g, align_bytes=64) for g in range(2)]
-        w1_scales = [held.tile([P, 512], U8, name="w1_scales%d" % g, align_bytes=64) for g in range(2)]
-        w2_codes = [held.tile([P, N], U32, name="w2_codes%d" % g, align_bytes=64) for g in range(2)]
-        w2_scales = [held.tile([P, N], U8, name="w2_scales%d" % g, align_bytes=64) for g in range(2)]
-        h_bf = [[held.tile([P, P, 4], BF16, name="h_bf%d%d" % (g, n), align_bytes=64) for n in range(2)] for g in range(2)]
-        h_own = [held.tile([P, P], U32, name="h_codes%d" % n, align_bytes=64) for n in range(2)]
-        h_codes = [[x_codes[:, P * n : P * n + P] for n in range(2)], [h_own[n][:] for n in range(2)]]
-        h_own_scales = [held.tile([P, P], U8, name="h_scales%d" % n, align_bytes=64) for n in range(2)]
-        h_scales = [[x_scales[:, P * n : P * n + P] for n in range(2)], [h_own_scales[n][:] for n in range(2)]]
-        out_sb = [[held.tile([P, P], F32, name="out_sb%d%d" % (m, n)) for n in range(2)] for m in range(2)]
+        offsets = held.tile([P, L * V // 16], U16, name="offsets")
+        w1a_raw = sb([P, 4, 512], F32, "w1a_raw")
+        shared = sb([P, 1280], F32, "shared")
+        w1b_raw = [shared[:, 256:1280].rearrange("p (j c) -> p j c", j=2), sb([P, 2, 512], F32, "w1b_raw1")]
+        x01 = sb([P, 2, T], F32, "x01")
+        x2 = sb([P, T], F32, "x2")
+        x3 = sb([P, T], F32, "x3")
+        w2_raw = [sb([P, 4, N], F32, "w2_raw%d" % g) for g in range(2)]
+
+        x_bf = sb([P, V, 4], BF16, "x_bf")
+        x_codes = [sb([P, P], U32, "x_codes%d" % n) for n in range(2)]
+        x_scales = [sb([P, P], U8, "x_scales%d" % n) for n in range(2)]
+        w1_bf = [sb([P, 2048], BF16, "w1_bf%d" % g) for g in range(2)]
+        w1_codes = [sb([P, 512], U32, "w1_codes%d" % g) for g in range(2)]
+        w1_scales = [sb([P, 512], U8, "w1_scales%d" % g) for g in range(2)]
+        w2_bf = [sb([P, N, 4], BF16, "w2_bf%d" % g) for g in range(2)]
+        w2_codes = [sb([P, N], U32, "w2_codes%d" % g) for g in range(2)]
+        w2_scales = [sb([P, N], U8, "w2_scales%d" % g) for g in range(2)]
+        h_bf = [[sb([P, P, 4], BF16, "h_bf%d%d" % (g, n)) for n in range(2)] for g in range(2)]
+        h_codes = [[sb([P, P], U32, "h_codes%d%d" % (g, n)) for n in range(2)] for g in range(2)]
+        h_scales = [[sb([P, P], U8, "h_scales%d%d" % (g, n)) for n in range(2)] for g in range(2)]
+        out_first = sb([P, V], F32, "out_first")
+        out_sb = [sb([P, P], F32, "out_sb%d" % n) for n in range(2)]
+        h0_bf = shared[:, 0:512].bitcast(BF16).rearrange("p (n j) -> p n j", j=4)
+        h0_scales = sb([P, V], U8, "h0_scales")
+        h0_codes = sb([P, V], U32, "h0_codes")
+        h_bf[0] = [h0_bf[:, P * n : P * n + P, :] for n in range(2)]
+        h_codes[0] = [h0_codes[:, P * n : P * n + P] for n in range(2)]
+        h_scales[0] = [h0_scales[:, P * n : P * n + P] for n in range(2)]
         h_ps = [[psum.tile([P, 4, P], F32, name="h_ps%d%d" % (g, n)) for n in range(2)] for g in range(2)]
         out_ps = [[psum.tile([P, 512], F32, name="out_ps%d%d" % (m, n)) for n in range(2)] for m in range(2)]
         warm = held.tile([P, 2], F32, name="warm")
 
         w1_rows = w1.rearrange("(p j) c -> p j c", j=4)
         w2_rows = w2.rearrange("(g p j) c -> g p j c", g=2, j=4)
-        x_rows = xT.rearrange("(p l) c -> l p c", l=4)
+        x_rows = xT.rearrange("(p l) c -> p l c", l=4)
 
-        nc.sync.dma_start(offsets[:], offs)
         nc.sync.dma_start(w1a_raw[:], w1_rows[:, :, 0:512])
-        for l in range(L):
-            nc.sync.dma_start(level[l][:], x_rows[l])
+        nc.sync.dma_start(offsets[:], offs)
+        nc.sync.dma_start(x01[:], x_rows[:, 0:2, :])
+        nc.sync.dma_start(x2[:], x_rows[:, 2, :])
+        nc.sync.dma_start(x3[:], x_rows[:, 3, :])
         for i in range(2):
             nc.sync.dma_start(w1b_raw[i][:], w1_rows[:, 2 * i : 2 * i + 2, 512:1024])
         for g in range(2):
@@ -63,9 +75,24 @@ def tile_picked_grid_mlp_gelu_sub_l_kernel(tc, xT, w1, w2, offs, out):
 
         def cast_w1(copy, g, j0, raw, lo, hi):
             copy(
-                w1_bf[g].rearrange("p (t m j) -> p m t j", t=4, j=4)[:, lo:hi, :, j0 : j0 + raw.shape[1]],
+                w1_bf[g][:].rearrange("p (t m j) -> p m t j", t=4, j=4)[:, lo:hi, :, j0 : j0 + raw.shape[1]],
                 raw[:].rearrange("p j (m t) -> p m t j", t=4)[:, lo:hi],
             )
+
+        def cast_w1_tiles(copy, g, j0, raw, t0, t1):
+            copy(
+                w1_bf[g][:].rearrange("p (t m j) -> p m t j", t=4, j=4)[:, :, t0:t1, j0 : j0 + raw.shape[1]],
+                raw[:].rearrange("p j (m t) -> p m t j", t=4)[:, :, t0:t1],
+            )
+
+        def cast_w1_row_pair(i, t0, t1):
+            nc.vector.tensor_copy(
+                w1_bf[1][:].rearrange("p (t m e j) -> p m t e j", t=4, e=2, j=4)[:, :, t0:t1, :, 2 * i : 2 * i + 2],
+                w1b_raw[i][:].rearrange("p j (m e t) -> p m t e j", e=2, t=4)[:, :, t0:t1],
+            )
+
+        def cast_w2(copy, g, lo, hi):
+            copy(w2_bf[g][:, lo:hi, :], w2_raw[g][:].rearrange("p j c -> p c j")[:, lo:hi, :])
 
         def quantise_w1(g, half):
             w = slice(256 * half, 256 * half + 256)
@@ -75,67 +102,101 @@ def tile_picked_grid_mlp_gelu_sub_l_kernel(tc, xT, w1, w2, offs, out):
                 in_=w1_bf[g][:, 1024 * half : 1024 * half + 1024],
             )
 
-        def prepare_w2(g):
-            grouped = w1_bf[1 - g][:, 0:1024]
-            nc.vector.tensor_copy(grouped.rearrange("p (c j) -> p c j", j=4), w2_raw[g][:].rearrange("p j c -> p c j"))
-            nc.vector.quantize_mx(out=w2_codes[g][:].bitcast(FP8X4), scales=w2_scales[g][:], in_=grouped)
-
         def quantise(codes, scales, src):
-            nc.vector.quantize_mx(out=codes.bitcast(FP8X4), scales=scales, in_=src[:].rearrange("p n j -> p (n j)"))
+            nc.vector.quantize_mx(out=codes[:].bitcast(FP8X4), scales=scales[:], in_=src)
+
+        def flat(ap):
+            return ap.rearrange("p n j -> p (n j)")
+
+        def gather(l, window, lo, hi):
+            first = l * V + lo
+            nc.vector.tensor_copy(x_bf[:, lo:hi, l], window.indirect(offsets[:, first // 16 : (first + hi - lo) // 16]))
 
         def layer1(g, n):
-            v = slice(P * n, P * n + P)
             for t in range(4):
                 m = slice(P * t, P * t + P)
                 nc.tensor.matmul_mx(
                     out=h_ps[g][n][:, t, :],
                     lhsT=w1_codes[g][:, m].bitcast(FP8X4),
                     lhsT_scale=w1_scales[g][:, m],
-                    rhs=x_codes[:, v].bitcast(FP8X4),
-                    rhs_scale=x_scales[:, v],
+                    rhs=x_codes[n][:].bitcast(FP8X4),
+                    rhs_scale=x_scales[n][:],
                     start=True,
                     stop=True,
                 )
+
+        def gelu(g, n):
             nc.scalar.activation(h_bf[g][n][:], h_ps[g][n][:].rearrange("p t n -> p n t"), GELU)
 
-        def layer2(g, n):
-            for mt in range(2):
-                m = slice(P * mt, P * mt + P)
-                nc.tensor.matmul_mx(
-                    out=out_ps[mt][n][:, 0:P],
-                    lhsT=w2_codes[g][:, m].bitcast(FP8X4),
-                    lhsT_scale=w2_scales[g][:, m],
-                    rhs=h_codes[g][n].bitcast(FP8X4),
-                    rhs_scale=h_scales[g][n],
-                    start=(g == 0),
-                    stop=(g == 1),
-                )
+        def quantise_h(g, n):
+            quantise(h_codes[g][n], h_scales[g][n], flat(h_bf[g][n][:]))
 
-        cast_w1(nc.vector.tensor_copy, 0, 0, w1a_raw, 0, 72)
-        cast_w1(nc.scalar.copy, 0, 0, w1a_raw, 72, 128)
-        for half in range(2):
-            quantise_w1(0, half)
-        for l in range(L):
-            nc.vector.tensor_copy(x_bf[:, :, l], level[l][:].indirect(offsets[:, 16 * l : 16 * l + 16]))
-        quantise(x_codes[:], x_scales[:], x_bf)
+        def layer2(g, n, mt):
+            m = slice(P * mt, P * mt + P)
+            nc.tensor.matmul_mx(
+                out=out_ps[mt][n][:, 0:P],
+                lhsT=w2_codes[g][:, m].bitcast(FP8X4),
+                lhsT_scale=w2_scales[g][:, m],
+                rhs=h_codes[g][n][:].bitcast(FP8X4),
+                rhs_scale=h_scales[g][n][:],
+                start=(g == 0),
+                stop=(g == 1),
+            )
+
+        vcopy, scopy = nc.vector.tensor_copy, nc.scalar.copy
+        cast_w1_tiles(vcopy, 0, 0, w1a_raw, 0, 2)
+        cast_w1_tiles(scopy, 0, 0, w1a_raw, 2, 4)
+        quantise(w1_codes[0], w1_scales[0], w1_bf[0][:])
+        gather(0, x01[:, 0, :], 0, V)
+        gather(1, x01[:, 1, :], 0, V)
+        gather(2, x2[:], 0, V)
+        for n in range(2):
+            gather(3, x3[:], P * n, P * n + P)
+            quantise(x_codes[n], x_scales[n], flat(x_bf[:, P * n : P * n + P, :]))
         for n in range(2):
             layer1(0, n)
-        for i in range(2):
-            cast_w1(nc.vector.tensor_copy, 1, 2 * i, w1b_raw[i], 0, 128)
+        for t in range(6):
+            nc.tensor.matmul_mx(
+                out=out_ps[t % 2][t // 2 % 2][:, P * (1 + t // 4) : P * (2 + t // 4)],
+                lhsT=w1_codes[0][:, 0:P].bitcast(FP8X4),
+                lhsT_scale=w1_scales[0][:, 0:P],
+                rhs=x_codes[1][:].bitcast(FP8X4),
+                rhs_scale=x_scales[1][:],
+                start=True,
+                stop=True,
+            )
+        cast_w1_row_pair(0, 0, 4)
+        for n in range(2):
+            gelu(0, n)
+        for half in range(2):
+            cast_w1_row_pair(1, 2 * half, 2 * half + 2)
         for half in range(2):
             quantise_w1(1, half)
         for n in range(2):
             layer1(1, n)
+        cast_w2(scopy, 0, 88, 256)
+        cast_w2(vcopy, 0, 0, 88)
+        quantise(w2_codes[0], w2_scales[0], flat(w2_bf[0][:]))
+        gelu(1, 0)
+        gelu(1, 1)
+        nc.vector.quantize_mx(out=h0_codes[:].bitcast(FP8X4), scales=h0_scales[:], in_=flat(h0_bf[:]))
         for n in range(2):
-            quantise(h_codes[0][n], h_scales[0][n], h_bf[0][n])
-        for g in range(2):
-            prepare_w2(g)
+            for mt in range(2):
+                layer2(0, n, mt)
         for n in range(2):
-            layer2(0, n)
-        for n in range(2):
-            quantise(h_codes[1][n], h_scales[1][n], h_bf[1][n])
-            layer2(1, n)
-            nc.vector.tensor_copy(out_sb[0][n][:], out_ps[0][n][:, 0:P])
-            nc.scalar.copy(out_sb[1][n][:], out_ps[1][n][:, 0:P])
-            nc.sync.dma_start(out[0:P, P * n : P * n + P], out_sb[0][n][:])
-            nc.scalar.dma_start(out[P : 2 * P, P * n : P * n + P], out_sb[1][n][:])
+            quantise_h(1, n)
+        cast_w2(vcopy, 1, 0, P)
+        cast_w2(scopy, 1, 160, N)
+        cast_w2(vcopy, 1, P, 160)
+        for mt in range(2):
+            m = slice(P * mt, P * mt + P)
+            quantise(w2_codes[1][:, m], w2_scales[1][:, m], flat(w2_bf[1][:, m, :]))
+            for n in range(2):
+                layer2(1, n, mt)
+        nc.scalar.copy(out_first[:, 0:P], out_ps[0][0][:, 0:P])
+        nc.vector.tensor_copy(out_first[:, P : 2 * P], out_ps[0][1][:, 0:P])
+        nc.sync.dma_start(out[0:P, :], out_first[:])
+        nc.scalar.copy(out_sb[0][:], out_ps[1][0][:, 0:P])
+        nc.vector.tensor_copy(out_sb[1][:], out_ps[1][1][:, 0:P])
+        nc.scalar.dma_start(out[P : 2 * P, 0:P], out_sb[0][:])
+        nc.sync.dma_start(out[P : 2 * P, P : 2 * P], out_sb[1][:])

@@ -27,7 +27,8 @@ def tile_picked_grid_mlp_gelu_sub_l_kernel(tc, xT, w1, w2, offs, out):
         w1a_raw = sb([P, 4, 512], F32, "w1a_raw")
         shared = sb([P, 1280], F32, "shared")
         w1b_raw = [shared[:, 256:1280].rearrange("p (j c) -> p j c", j=2), sb([P, 2, 512], F32, "w1b_raw1")]
-        x01 = sb([P, 2, T], F32, "x01")
+        x0 = sb([P, T], F32, "x0")
+        x1 = sb([P, T], F32, "x1")
         x2 = sb([P, T], F32, "x2")
         x3 = sb([P, T], F32, "x3")
         w2_raw = [sb([P, 4, N], F32, "w2_raw%d" % g) for g in range(2)]
@@ -60,9 +61,10 @@ def tile_picked_grid_mlp_gelu_sub_l_kernel(tc, xT, w1, w2, offs, out):
         w2_rows = w2.rearrange("(g p j) c -> g p j c", g=2, j=4)
         x_rows = xT.rearrange("(p l) c -> p l c", l=4)
 
-        nc.sync.dma_start(w1a_raw[:], w1_rows[:, :, 0:512])
         nc.sync.dma_start(offsets[:], offs)
-        nc.sync.dma_start(x01[:], x_rows[:, 0:2, :])
+        nc.sync.dma_start(w1a_raw[:], w1_rows[:, :, 0:512])
+        nc.sync.dma_start(x0[:], x_rows[:, 0, :])
+        nc.sync.dma_start(x1[:], x_rows[:, 1, :])
         nc.sync.dma_start(x2[:], x_rows[:, 2, :])
         nc.sync.dma_start(x3[:], x_rows[:, 3, :])
         for i in range(2):
@@ -147,8 +149,8 @@ def tile_picked_grid_mlp_gelu_sub_l_kernel(tc, xT, w1, w2, offs, out):
         cast_w1_tiles(vcopy, 0, 0, w1a_raw, 0, 2)
         cast_w1_tiles(scopy, 0, 0, w1a_raw, 2, 4)
         quantise(w1_codes[0], w1_scales[0], w1_bf[0][:])
-        gather(0, x01[:, 0, :], 0, V)
-        gather(1, x01[:, 1, :], 0, V)
+        gather(0, x0[:], 0, V)
+        gather(1, x1[:], 0, V)
         gather(2, x2[:], 0, V)
         for n in range(2):
             gather(3, x3[:], P * n, P * n + P)
@@ -174,8 +176,8 @@ def tile_picked_grid_mlp_gelu_sub_l_kernel(tc, xT, w1, w2, offs, out):
             quantise_w1(1, half)
         for n in range(2):
             layer1(1, n)
-        cast_w2(scopy, 0, 88, 256)
-        cast_w2(vcopy, 0, 0, 88)
+        cast_w2(scopy, 0, 64, 256)
+        cast_w2(vcopy, 0, 0, 64)
         quantise(w2_codes[0], w2_scales[0], flat(w2_bf[0][:]))
         gelu(1, 0)
         gelu(1, 1)
@@ -186,8 +188,7 @@ def tile_picked_grid_mlp_gelu_sub_l_kernel(tc, xT, w1, w2, offs, out):
         for n in range(2):
             quantise_h(1, n)
         cast_w2(vcopy, 1, 0, P)
-        cast_w2(scopy, 1, 160, N)
-        cast_w2(vcopy, 1, P, 160)
+        cast_w2(vcopy, 1, P, 256)
         for mt in range(2):
             m = slice(P * mt, P * mt + P)
             quantise(w2_codes[1][:, m], w2_scales[1][:, m], flat(w2_bf[1][:, m, :]))

@@ -63,7 +63,7 @@ def tile_picked_grid_mlp_gelu_sub_l_kernel(tc, xT, w1, w2, offs, out):
 
         nc.sync.dma_start(offsets[:], offs)
         nc.sync.dma_start(w1a_raw[:], w1_rows[:, :, 0:512])
-        nc.sync.dma_start(x0[:], x_rows[:, 0, :])
+        nc.scalar.dma_start(x0[:], x_rows[:, 0, :])
         nc.sync.dma_start(x1[:], x_rows[:, 1, :])
         nc.sync.dma_start(x2[:], x_rows[:, 2, :])
         nc.sync.dma_start(x3[:], x_rows[:, 3, :])
@@ -157,13 +157,13 @@ def tile_picked_grid_mlp_gelu_sub_l_kernel(tc, xT, w1, w2, offs, out):
             quantise(x_codes[n], x_scales[n], flat(x_bf[:, P * n : P * n + P, :]))
         for n in range(2):
             layer1(0, n)
-        for t in range(6):
+        for t in range(2):
             nc.tensor.matmul_mx(
-                out=out_ps[t % 2][t // 2 % 2][:, P * (1 + t // 4) : P * (2 + t // 4)],
-                lhsT=w1_codes[0][:, 0:P].bitcast(FP8X4),
-                lhsT_scale=w1_scales[0][:, 0:P],
-                rhs=x_codes[1][:].bitcast(FP8X4),
-                rhs_scale=x_scales[1][:],
+                out=out_ps[t][1][0:64, :],
+                lhsT=x_codes[1][:, 0:64].bitcast(FP8X4),
+                lhsT_scale=x_scales[1][:, 0:64],
+                rhs=w1_codes[0][:].bitcast(FP8X4),
+                rhs_scale=w1_scales[0][:],
                 start=True,
                 stop=True,
             )

@@ -94,7 +94,10 @@ def tile_picked_grid_mlp_gelu_sub_l_kernel(tc, xT, w1, w2, offs, out):
             )
 
         def cast_w2(copy, g, lo, hi):
-            copy(w2_bf[g][:, lo:hi, :], w2_raw[g][:].rearrange("p j c -> p c j")[:, lo:hi, :])
+            copy(
+                w2_bf[g][:, lo:hi, :].rearrange("p (c i) j -> p c j i", i=4),
+                w2_raw[g][:, :, lo:hi].rearrange("p j (c i) -> p c j i", i=4),
+            )
 
         def quantise_w1(g, half):
             w = slice(256 * half, 256 * half + 256)

@@ -31,7 +31,10 @@ def tile_picked_grid_mlp_gelu_sub_l_kernel(tc, xT, w1, w2, offs, out):
         x1 = sb([P, T], F32, "x1")
         x2 = sb([P, T], F32, "x2")
         x3 = sb([P, T], F32, "x3")
-        w2_raw = [sb([P, 4, N], F32, "w2_raw%d" % g) for g in range(2)]
+        w2_raw = [sb([P, 4, N], F32, "w2a_raw"), held.tile([P, 4, N], F32, name="w2b_raw", tag="last_load", align_bytes=64)]
+        tail_bf = sb([P, P + N, 4], BF16, "tail_bf")
+        tail_codes = sb([P, P + N], U32, "tail_codes")
+        tail_scales = sb([P, P + N], U8, "tail_scales")
 
         x_bf = sb([P, V, 4], BF16, "x_bf")
         x_codes = [sb([P, P], U32, "x_codes%d" % n) for n in range(2)]
@@ -53,6 +56,8 @@ def tile_picked_grid_mlp_gelu_sub_l_kernel(tc, xT, w1, w2, offs, out):
         h_bf[0] = [h0_bf[:, P * n : P * n + P, :] for n in range(2)]
         h_codes[0] = [h0_codes[:, P * n : P * n + P] for n in range(2)]
         h_scales[0] = [h0_scales[:, P * n : P * n + P] for n in range(2)]
+        w2_bf[1], w2_codes[1], w2_scales[1] = tail_bf[:, P:, :], tail_codes[:, P:], tail_scales[:, P:]
+        h_bf[1][0], h_codes[1][0], h_scales[1][0] = tail_bf[:, 0:P, :], tail_codes[:, 0:P], tail_scales[:, 0:P]
         h_ps = [[psum.tile([P, 4, P], F32, name="h_ps%d%d" % (g, n)) for n in range(2)] for g in range(2)]
         out_ps = [[psum.tile([P, 512], F32, name="out_ps%d%d" % (m, n)) for n in range(2)] for m in range(2)]
         warm = held.tile([P, 2], F32, name="warm")
@@ -188,19 +193,20 @@ def tile_picked_grid_mlp_gelu_sub_l_kernel(tc, xT, w1, w2, offs, out):
         for n in range(2):
             for mt in range(2):
                 layer2(0, n, mt)
-        for n in range(2):
-            quantise_h(1, n)
         cast_w2(vcopy, 1, 0, P)
         cast_w2(vcopy, 1, P, 256)
-        for mt in range(2):
-            m = slice(P * mt, P * mt + P)
-            quantise(w2_codes[1][:, m], w2_scales[1][:, m], flat(w2_bf[1][:, m, :]))
-            for n in range(2):
+        quantise(tail_codes[:, 0:256], tail_scales[:, 0:256], flat(tail_bf[:, 0:256, :]))
+        quantise(tail_codes[:, 256:384], tail_scales[:, 256:384], flat(tail_bf[:, 256:384, :]))
+        h_codes[1][1] = held.tile([P, P], U32, name="last_codes", tag="last_load", align_bytes=64)
+        quantise_h(1, 1)
+        for n in range(2):
+            for mt in range(2):
                 layer2(1, n, mt)
+        out_halves = out.rearrange("(mt p) v -> p mt v", mt=2)
         nc.scalar.copy(out_first[:, 0:P], out_ps[0][0][:, 0:P])
-        nc.vector.tensor_copy(out_first[:, P : 2 * P], out_ps[0][1][:, 0:P])
-        nc.sync.dma_start(out[0:P, :], out_first[:])
-        nc.scalar.copy(out_sb[0][:], out_ps[1][0][:, 0:P])
+        nc.vector.tensor_copy(out_first[:, P : 2 * P], out_ps[1][0][:, 0:P])
+        nc.sync.dma_start(out_halves[:, :, 0:P], out_first[:].rearrange("p (mt v) -> p mt v", mt=2))
+        nc.scalar.copy(out_sb[0][:], out_ps[0][1][:, 0:P])
         nc.vector.tensor_copy(out_sb[1][:], out_ps[1][1][:, 0:P])
-        nc.scalar.dma_start(out[P : 2 * P, 0:P], out_sb[0][:])
+        nc.scalar.dma_start(out[0:P, P : 2 * P], out_sb[0][:])
         nc.sync.dma_start(out[P : 2 * P, P : 2 * P], out_sb[1][:])

@@ -9,8 +9,13 @@ U16 = mybir.dt.uint16
 U8 = mybir.dt.uint8
 FP8X4 = mybir.dt.float8_e4m3fn_x4
 GELU = mybir.ActivationFunctionType.Gelu_apprx_tanh
+
 P = 128
 K, T, H, N, V, L = 512, 1024, 1024, 256, 256, 4
+PACK = 4
+PASS = P * PACK
+W2_VECTOR_COLUMNS = 64
+WARM_ROWS = 64
 FLOPS = 2 * V * (K * H + H * N)
 
 
@@ -23,112 +28,96 @@ def tile_picked_grid_mlp_gelu_sub_l_kernel(tc, xT, w1, w2, offs, out):
         def sb(shape, dtype, name):
             return held.tile(shape, dtype, name=name, align_bytes=64)
 
-        offsets = held.tile([P, L * V // 16], U16, name="offsets")
-        w1a_raw = sb([P, 4, 512], F32, "w1a_raw")
-        shared = sb([P, 1280], F32, "shared")
-        w1b_raw = [shared[:, 256:1280].rearrange("p (j c) -> p j c", j=2), sb([P, 2, 512], F32, "w1b_raw1")]
-        x0 = sb([P, T], F32, "x0")
-        x1 = sb([P, T], F32, "x1")
-        x2 = sb([P, T], F32, "x2")
-        x3 = sb([P, T], F32, "x3")
-        w2_raw = [sb([P, 4, N], F32, "w2a_raw"), held.tile([P, 4, N], F32, name="w2b_raw", tag="last_load", align_bytes=64)]
-        tail_bf = sb([P, P + N, 4], BF16, "tail_bf")
-        tail_codes = sb([P, P + N], U32, "tail_codes")
-        tail_scales = sb([P, P + N], U8, "tail_scales")
+        def in_last_load_slot(shape, dtype, name):
+            return held.tile(shape, dtype, name=name, tag="last_load", align_bytes=64)
 
-        x_bf = sb([P, V, 4], BF16, "x_bf")
+        offsets = held.tile([P, L * V // 16], U16, name="offsets")
+        w1_first_raw = sb([P, PACK, PASS], F32, "w1_first_raw")
+        shared = sb([P, V + 2 * PASS], F32, "shared")
+        h_first_bf = shared[:, 0 : 2 * V].bitcast(BF16).rearrange("p (v j) -> p v j", j=PACK)
+        w1_pair_raw = [shared[:, V:].rearrange("p (j c) -> p j c", j=2), sb([P, 2, PASS], F32, "w1_last_pair_raw")[:]]
+        x_raw = [sb([P, T], F32, "x_raw%d" % l) for l in range(L)]
+        w2_raw = [sb([P, PACK, N], F32, "w2_first_raw"), in_last_load_slot([P, PACK, N], F32, "w2_last_raw")]
+
+        x_bf = sb([P, V, PACK], BF16, "x_bf")
         x_codes = [sb([P, P], U32, "x_codes%d" % n) for n in range(2)]
         x_scales = [sb([P, P], U8, "x_scales%d" % n) for n in range(2)]
-        w1_bf = [sb([P, 2048], BF16, "w1_bf%d" % g) for g in range(2)]
-        w1_codes = [sb([P, 512], U32, "w1_codes%d" % g) for g in range(2)]
-        w1_scales = [sb([P, 512], U8, "w1_scales%d" % g) for g in range(2)]
-        w2_bf = [sb([P, N, 4], BF16, "w2_bf%d" % g) for g in range(2)]
-        w2_codes = [sb([P, N], U32, "w2_codes%d" % g) for g in range(2)]
-        w2_scales = [sb([P, N], U8, "w2_scales%d" % g) for g in range(2)]
-        h_bf = [[sb([P, P, 4], BF16, "h_bf%d%d" % (g, n)) for n in range(2)] for g in range(2)]
-        h_codes = [[sb([P, P], U32, "h_codes%d%d" % (g, n)) for n in range(2)] for g in range(2)]
-        h_scales = [[sb([P, P], U8, "h_scales%d%d" % (g, n)) for n in range(2)] for g in range(2)]
-        out_first = sb([P, V], F32, "out_first")
-        out_sb = [sb([P, P], F32, "out_sb%d" % n) for n in range(2)]
-        h0_bf = shared[:, 0:512].bitcast(BF16).rearrange("p (n j) -> p n j", j=4)
-        h0_scales = sb([P, V], U8, "h0_scales")
-        h0_codes = sb([P, V], U32, "h0_codes")
-        h_bf[0] = [h0_bf[:, P * n : P * n + P, :] for n in range(2)]
-        h_codes[0] = [h0_codes[:, P * n : P * n + P] for n in range(2)]
-        h_scales[0] = [h0_scales[:, P * n : P * n + P] for n in range(2)]
-        w2_bf[1], w2_codes[1], w2_scales[1] = tail_bf[:, P:, :], tail_codes[:, P:], tail_scales[:, P:]
-        h_bf[1][0], h_codes[1][0], h_scales[1][0] = tail_bf[:, 0:P, :], tail_codes[:, 0:P], tail_scales[:, 0:P]
-        h_ps = [[psum.tile([P, 4, P], F32, name="h_ps%d%d" % (g, n)) for n in range(2)] for g in range(2)]
-        out_ps = [[psum.tile([P, 512], F32, name="out_ps%d%d" % (m, n)) for n in range(2)] for m in range(2)]
-        warm = held.tile([P, 2], F32, name="warm")
+        w1_bf = [sb([P, PASS * PACK], BF16, "w1_bf%d" % g) for g in range(2)]
+        w1_codes = [sb([P, PASS], U32, "w1_codes%d" % g) for g in range(2)]
+        w1_scales = [sb([P, PASS], U8, "w1_scales%d" % g) for g in range(2)]
+        w2_first_bf = sb([P, N, PACK], BF16, "w2_first_bf")
+        w2_first_codes = sb([P, N], U32, "w2_first_codes")
+        w2_first_scales = sb([P, N], U8, "w2_first_scales")
+        h_first_codes = sb([P, V], U32, "h_first_codes")
+        h_first_scales = sb([P, V], U8, "h_first_scales")
+        tail_bf = sb([P, P + N, PACK], BF16, "tail_bf")
+        tail_codes = sb([P, P + N], U32, "tail_codes")
+        tail_scales = sb([P, P + N], U8, "tail_scales")
+        h_last_bf = sb([P, P, PACK], BF16, "h_last_bf")
+        h_last_scales = sb([P, P], U8, "h_last_scales")
+        out_sb = [[sb([P, P], F32, "out_sb%d%d" % (r, n)) for n in range(2)] for r in range(2)]
 
-        w1_rows = w1.rearrange("(p j) c -> p j c", j=4)
-        w2_rows = w2.rearrange("(g p j) c -> g p j c", g=2, j=4)
-        x_rows = xT.rearrange("(p l) c -> p l c", l=4)
+        h_ps = [[psum.tile([P, PACK, P], F32, name="h_ps%d%d" % (g, n)) for n in range(2)] for g in range(2)]
+        out_ps = [[psum.tile([P, PASS], F32, name="out_ps%d%d" % (r, n)) for n in range(2)] for r in range(2)]
 
+        def half(i):
+            return slice(P * i, P * i + P)
+
+        w2_bf = [w2_first_bf[:], tail_bf[:, P:, :]]
+        w2_codes = [w2_first_codes[:], tail_codes[:, P:]]
+        w2_scales = [w2_first_scales[:], tail_scales[:, P:]]
+        h_bf = [[h_first_bf[:, half(n), :] for n in range(2)], [tail_bf[:, half(0), :], h_last_bf[:]]]
+        h_scales = [[h_first_scales[:, half(n)] for n in range(2)], [tail_scales[:, half(0)], h_last_scales[:]]]
+
+        w1_rows = w1.rearrange("(p j) c -> p j c", j=PACK)
+        w2_rows = w2.rearrange("(g p j) c -> g p j c", g=2, j=PACK)
+        x_rows = xT.rearrange("(p l) c -> p l c", l=L)
         nc.sync.dma_start(offsets[:], offs)
-        nc.sync.dma_start(w1a_raw[:], w1_rows[:, :, 0:512])
-        nc.scalar.dma_start(x0[:], x_rows[:, 0, :])
-        nc.sync.dma_start(x1[:], x_rows[:, 1, :])
-        nc.sync.dma_start(x2[:], x_rows[:, 2, :])
-        nc.sync.dma_start(x3[:], x_rows[:, 3, :])
-        for i in range(2):
-            nc.sync.dma_start(w1b_raw[i][:], w1_rows[:, 2 * i : 2 * i + 2, 512:1024])
+        nc.sync.dma_start(w1_first_raw[:], w1_rows[:, :, 0:PASS])
+        nc.scalar.dma_start(x_raw[0][:], x_rows[:, 0, :])
+        for l in range(1, L):
+            nc.sync.dma_start(x_raw[l][:], x_rows[:, l, :])
+        for pair in range(2):
+            nc.sync.dma_start(w1_pair_raw[pair], w1_rows[:, 2 * pair : 2 * pair + 2, PASS:H])
         for g in range(2):
             nc.sync.dma_start(w2_raw[g][:], w2_rows[g])
 
-        nc.vector.memset(warm[:], 0.0)
-        nc.scalar.activation(warm[:, 1:2], warm[:, 0:1], GELU)
-
-        def cast_w1(copy, g, j0, raw, lo, hi):
+        def round_w1_first_half(copy, t0, t1):
             copy(
-                w1_bf[g][:].rearrange("p (t m j) -> p m t j", t=4, j=4)[:, lo:hi, :, j0 : j0 + raw.shape[1]],
-                raw[:].rearrange("p j (m t) -> p m t j", t=4)[:, lo:hi],
+                w1_bf[0][:].rearrange("p (t m j) -> p m t j", t=PACK, j=PACK)[:, :, t0:t1],
+                w1_first_raw[:].rearrange("p j (m t) -> p m t j", t=PACK)[:, :, t0:t1],
             )
 
-        def cast_w1_tiles(copy, g, j0, raw, t0, t1):
-            copy(
-                w1_bf[g][:].rearrange("p (t m j) -> p m t j", t=4, j=4)[:, :, t0:t1, j0 : j0 + raw.shape[1]],
-                raw[:].rearrange("p j (m t) -> p m t j", t=4)[:, :, t0:t1],
-            )
-
-        def cast_w1_row_pair(i, t0, t1):
+        def round_w1_row_pair(pair, t0, t1):
+            slots = slice(2 * pair, 2 * pair + 2)
             nc.vector.tensor_copy(
-                w1_bf[1][:].rearrange("p (t m e j) -> p m t e j", t=4, e=2, j=4)[:, :, t0:t1, :, 2 * i : 2 * i + 2],
-                w1b_raw[i][:].rearrange("p j (m e t) -> p m t e j", e=2, t=4)[:, :, t0:t1],
+                w1_bf[1][:].rearrange("p (t q e j) -> p q t e j", t=PACK, e=2, j=PACK)[:, :, t0:t1, :, slots],
+                w1_pair_raw[pair].rearrange("p j (q e t) -> p q t e j", e=2, t=PACK)[:, :, t0:t1],
             )
 
-        def cast_w2(copy, g, lo, hi):
+        def round_w2(copy, g, lo, hi):
             copy(
-                w2_bf[g][:, lo:hi, :].rearrange("p (c i) j -> p c j i", i=4),
-                w2_raw[g][:, :, lo:hi].rearrange("p j (c i) -> p c j i", i=4),
+                w2_bf[g][:, lo:hi, :].rearrange("p (c e) j -> p c j e", e=4),
+                w2_raw[g][:, :, lo:hi].rearrange("p j (c e) -> p c j e", e=4),
             )
-
-        def quantise_w1(g, half):
-            w = slice(256 * half, 256 * half + 256)
-            nc.vector.quantize_mx(
-                out=w1_codes[g][:, w].bitcast(FP8X4),
-                scales=w1_scales[g][:, w],
-                in_=w1_bf[g][:, 1024 * half : 1024 * half + 1024],
-            )
-
-        def quantise(codes, scales, src):
-            nc.vector.quantize_mx(out=codes[:].bitcast(FP8X4), scales=scales[:], in_=src)
 
         def flat(ap):
-            return ap.rearrange("p n j -> p (n j)")
+            return ap.rearrange("p c j -> p (c j)")
 
-        def gather(l, window, lo, hi):
+        def quantise(codes, scales, rounded):
+            nc.vector.quantize_mx(out=codes.bitcast(FP8X4), scales=scales, in_=rounded)
+
+        def look_up(l, lo, hi):
             first = l * V + lo
-            nc.vector.tensor_copy(x_bf[:, lo:hi, l], window.indirect(offsets[:, first // 16 : (first + hi - lo) // 16]))
+            entries = offsets[:, first // 16 : (first + hi - lo) // 16]
+            nc.vector.tensor_copy(x_bf[:, lo:hi, l], x_raw[l][:].indirect(entries))
 
-        def layer1(g, n):
-            for t in range(4):
-                m = slice(P * t, P * t + P)
+        def first_layer(g, n):
+            for t in range(PACK):
                 nc.tensor.matmul_mx(
                     out=h_ps[g][n][:, t, :],
-                    lhsT=w1_codes[g][:, m].bitcast(FP8X4),
-                    lhsT_scale=w1_scales[g][:, m],
+                    lhsT=w1_codes[g][:, half(t)].bitcast(FP8X4),
+                    lhsT_scale=w1_scales[g][:, half(t)],
                     rhs=x_codes[n][:].bitcast(FP8X4),
                     rhs_scale=x_scales[n][:],
                     start=True,
@@ -136,77 +125,75 @@ def tile_picked_grid_mlp_gelu_sub_l_kernel(tc, xT, w1, w2, offs, out):
                 )
 
         def gelu(g, n):
-            nc.scalar.activation(h_bf[g][n][:], h_ps[g][n][:].rearrange("p t n -> p n t"), GELU)
+            nc.scalar.activation(h_bf[g][n], h_ps[g][n][:].rearrange("p t v -> p v t"), GELU)
 
-        def quantise_h(g, n):
-            quantise(h_codes[g][n], h_scales[g][n], flat(h_bf[g][n][:]))
+        def second_layer(g, n, h_codes):
+            for r in range(2):
+                nc.tensor.matmul_mx(
+                    out=out_ps[r][n][:, 0:P],
+                    lhsT=w2_codes[g][:, half(r)].bitcast(FP8X4),
+                    lhsT_scale=w2_scales[g][:, half(r)],
+                    rhs=h_codes.bitcast(FP8X4),
+                    rhs_scale=h_scales[g][n],
+                    start=(g == 0),
+                    stop=(g == 1),
+                )
 
-        def layer2(g, n, mt):
-            m = slice(P * mt, P * mt + P)
-            nc.tensor.matmul_mx(
-                out=out_ps[mt][n][:, 0:P],
-                lhsT=w2_codes[g][:, m].bitcast(FP8X4),
-                lhsT_scale=w2_scales[g][:, m],
-                rhs=h_codes[g][n][:].bitcast(FP8X4),
-                rhs_scale=h_scales[g][n][:],
-                start=(g == 0),
-                stop=(g == 1),
-            )
+        on_vector, on_scalar = nc.vector.tensor_copy, nc.scalar.copy
 
-        vcopy, scopy = nc.vector.tensor_copy, nc.scalar.copy
-        cast_w1_tiles(vcopy, 0, 0, w1a_raw, 0, 2)
-        cast_w1_tiles(scopy, 0, 0, w1a_raw, 2, 4)
-        quantise(w1_codes[0], w1_scales[0], w1_bf[0][:])
-        gather(0, x0[:], 0, V)
-        gather(1, x1[:], 0, V)
-        gather(2, x2[:], 0, V)
+        round_w1_first_half(on_vector, 0, 2)
+        round_w1_first_half(on_scalar, 2, PACK)
+        quantise(w1_codes[0][:], w1_scales[0][:], w1_bf[0][:])
+        for l in range(L - 1):
+            look_up(l, 0, V)
         for n in range(2):
-            gather(3, x3[:], P * n, P * n + P)
-            quantise(x_codes[n], x_scales[n], flat(x_bf[:, P * n : P * n + P, :]))
+            look_up(L - 1, P * n, P * n + P)
+            quantise(x_codes[n][:], x_scales[n][:], flat(x_bf[:, half(n), :]))
         for n in range(2):
-            layer1(0, n)
-        for t in range(2):
+            first_layer(0, n)
+        for r in range(2):
             nc.tensor.matmul_mx(
-                out=out_ps[t][1][0:64, :],
-                lhsT=x_codes[1][:, 0:64].bitcast(FP8X4),
-                lhsT_scale=x_scales[1][:, 0:64],
+                out=out_ps[r][1][0:WARM_ROWS, :],
+                lhsT=x_codes[1][:, 0:WARM_ROWS].bitcast(FP8X4),
+                lhsT_scale=x_scales[1][:, 0:WARM_ROWS],
                 rhs=w1_codes[0][:].bitcast(FP8X4),
                 rhs_scale=w1_scales[0][:],
                 start=True,
                 stop=True,
             )
-        cast_w1_row_pair(0, 0, 4)
+        round_w1_row_pair(0, 0, PACK)
         for n in range(2):
             gelu(0, n)
-        for half in range(2):
-            cast_w1_row_pair(1, 2 * half, 2 * half + 2)
-        for half in range(2):
-            quantise_w1(1, half)
+
+        for i in range(2):
+            round_w1_row_pair(1, 2 * i, 2 * i + 2)
+        for i in range(2):
+            columns = slice(2 * P * i, 2 * P * i + 2 * P)
+            values = slice(2 * PASS * i, 2 * PASS * i + 2 * PASS)
+            quantise(w1_codes[1][:, columns], w1_scales[1][:, columns], w1_bf[1][:, values])
         for n in range(2):
-            layer1(1, n)
-        cast_w2(scopy, 0, 64, 256)
-        cast_w2(vcopy, 0, 0, 64)
-        quantise(w2_codes[0], w2_scales[0], flat(w2_bf[0][:]))
-        gelu(1, 0)
-        gelu(1, 1)
-        nc.vector.quantize_mx(out=h0_codes[:].bitcast(FP8X4), scales=h0_scales[:], in_=flat(h0_bf[:]))
+            first_layer(1, n)
+
+        round_w2(on_scalar, 0, W2_VECTOR_COLUMNS, N)
+        round_w2(on_vector, 0, 0, W2_VECTOR_COLUMNS)
+        quantise(w2_codes[0], w2_scales[0], flat(w2_bf[0]))
         for n in range(2):
-            for mt in range(2):
-                layer2(0, n, mt)
-        cast_w2(vcopy, 1, 0, P)
-        cast_w2(vcopy, 1, P, 256)
-        quantise(tail_codes[:, 0:256], tail_scales[:, 0:256], flat(tail_bf[:, 0:256, :]))
-        quantise(tail_codes[:, 256:384], tail_scales[:, 256:384], flat(tail_bf[:, 256:384, :]))
-        h_codes[1][1] = held.tile([P, P], U32, name="last_codes", tag="last_load", align_bytes=64)
-        quantise_h(1, 1)
+            gelu(1, n)
+        quantise(h_first_codes[:], h_first_scales[:], flat(h_first_bf))
         for n in range(2):
-            for mt in range(2):
-                layer2(1, n, mt)
-        out_halves = out.rearrange("(mt p) v -> p mt v", mt=2)
-        nc.scalar.copy(out_first[:, 0:P], out_ps[0][0][:, 0:P])
-        nc.vector.tensor_copy(out_first[:, P : 2 * P], out_ps[1][0][:, 0:P])
-        nc.sync.dma_start(out_halves[:, :, 0:P], out_first[:].rearrange("p (mt v) -> p mt v", mt=2))
-        nc.scalar.copy(out_sb[0][:], out_ps[0][1][:, 0:P])
-        nc.vector.tensor_copy(out_sb[1][:], out_ps[1][1][:, 0:P])
-        nc.scalar.dma_start(out[0:P, P : 2 * P], out_sb[0][:])
-        nc.sync.dma_start(out[P : 2 * P, P : 2 * P], out_sb[1][:])
+            second_layer(0, n, h_first_codes[:, half(n)])
+
+        for r in range(2):
+            round_w2(on_vector, 1, P * r, P * r + P)
+        for columns in (slice(0, 2 * P), slice(2 * P, P + N)):
+            quantise(tail_codes[:, columns], tail_scales[:, columns], flat(tail_bf[:, columns, :]))
+        h_last_codes = in_last_load_slot([P, P], U32, "h_last_codes")
+        quantise(h_last_codes[:], h_last_scales[:], flat(h_last_bf[:]))
+        second_layer(1, 0, tail_codes[:, half(0)])
+        second_layer(1, 1, h_last_codes[:])
+
+        for n in range(2):
+            nc.scalar.copy(out_sb[0][n][:], out_ps[0][n][:, 0:P])
+            (nc.scalar if n == 1 else nc.sync).dma_start(out[half(0), half(n)], out_sb[0][n][:])
+            nc.vector.tensor_copy(out_sb[1][n][:], out_ps[1][n][:, 0:P])
+            nc.sync.dma_start(out[half(1), half(n)], out_sb[1][n][:])

@@ -14,7 +14,7 @@ P = 128
 K, T, H, N, V, L = 512, 1024, 1024, 256, 256, 4
 PACK = 4
 PASS = P * PACK
-W2_VECTOR_COLUMNS = 64
+W2_VECTOR_COLUMNS = 192
 WARM_ROWS = 64
 FLOPS = 2 * V * (K * H + H * N)
 
@@ -35,7 +35,7 @@ def tile_picked_grid_mlp_gelu_sub_l_kernel(tc, xT, w1, w2, offs, out):
         w1_first_raw = sb([P, PACK, PASS], F32, "w1_first_raw")
         shared = sb([P, V + 2 * PASS], F32, "shared")
         h_first_bf = shared[:, 0 : 2 * V].bitcast(BF16).rearrange("p (v j) -> p v j", j=PACK)
-        w1_pair_raw = [shared[:, V:].rearrange("p (j c) -> p j c", j=2), sb([P, 2, PASS], F32, "w1_last_pair_raw")[:]]
+        w1_pair_raw = [sb([P, 2, PASS], F32, "w1_first_pair_raw")[:], shared[:, V:].rearrange("p (j c) -> p j c", j=2)]
         x_raw = [sb([P, T], F32, "x_raw%d" % l) for l in range(L)]
         w2_raw = [sb([P, PACK, N], F32, "w2_first_raw"), in_last_load_slot([P, PACK, N], F32, "w2_last_raw")]
 
@@ -88,11 +88,11 @@ def tile_picked_grid_mlp_gelu_sub_l_kernel(tc, xT, w1, w2, offs, out):
                 w1_first_raw[:].rearrange("p j (m t) -> p m t j", t=PACK)[:, :, t0:t1],
             )
 
-        def round_w1_row_pair(pair, t0, t1):
+        def round_w1_row_pair(copy, pair, t0, t1, q0=0, q1=P // 2):
             slots = slice(2 * pair, 2 * pair + 2)
-            nc.vector.tensor_copy(
-                w1_bf[1][:].rearrange("p (t q e j) -> p q t e j", t=PACK, e=2, j=PACK)[:, :, t0:t1, :, slots],
-                w1_pair_raw[pair].rearrange("p j (q e t) -> p q t e j", e=2, t=PACK)[:, :, t0:t1],
+            copy(
+                w1_bf[1][:].rearrange("p (t q e j) -> p q t e j", t=PACK, e=2, j=PACK)[:, q0:q1, t0:t1, :, slots],
+                w1_pair_raw[pair].rearrange("p j (q e t) -> p q t e j", e=2, t=PACK)[:, q0:q1, t0:t1],
             )
 
         def round_w2(copy, g, lo, hi):
@@ -106,6 +106,11 @@ def tile_picked_grid_mlp_gelu_sub_l_kernel(tc, xT, w1, w2, offs, out):
 
         def quantise(codes, scales, rounded):
             nc.vector.quantize_mx(out=codes.bitcast(FP8X4), scales=scales, in_=rounded)
+
+        def quantise_w1(g, i):
+            columns = slice(2 * P * i, 2 * P * i + 2 * P)
+            values = slice(2 * PASS * i, 2 * PASS * i + 2 * PASS)
+            quantise(w1_codes[g][:, columns], w1_scales[g][:, columns], w1_bf[g][:, values])
 
         def look_up(l, lo, hi):
             first = l * V + lo
@@ -143,7 +148,18 @@ def tile_picked_grid_mlp_gelu_sub_l_kernel(tc, xT, w1, w2, offs, out):
 
         round_w1_first_half(on_vector, 0, 2)
         round_w1_first_half(on_scalar, 2, PACK)
-        quantise(w1_codes[0][:], w1_scales[0][:], w1_bf[0][:])
+        for i in range(2):
+            quantise_w1(0, i)
+        for r in range(2):
+            nc.tensor.matmul_mx(
+                out=out_ps[r][1][0:WARM_ROWS, :],
+                lhsT=w1_codes[0][:, 0:WARM_ROWS].bitcast(FP8X4),
+                lhsT_scale=w1_scales[0][:, 0:WARM_ROWS],
+                rhs=w1_codes[0][:].bitcast(FP8X4),
+                rhs_scale=w1_scales[0][:],
+                start=True,
+                stop=True,
+            )
         for l in range(L - 1):
             look_up(l, 0, V)
         for n in range(2):
@@ -151,26 +167,15 @@ def tile_picked_grid_mlp_gelu_sub_l_kernel(tc, xT, w1, w2, offs, out):
             quantise(x_codes[n][:], x_scales[n][:], flat(x_bf[:, half(n), :]))
         for n in range(2):
             first_layer(0, n)
-        for r in range(2):
-            nc.tensor.matmul_mx(
-                out=out_ps[r][1][0:WARM_ROWS, :],
-                lhsT=x_codes[1][:, 0:WARM_ROWS].bitcast(FP8X4),
-                lhsT_scale=x_scales[1][:, 0:WARM_ROWS],
-                rhs=w1_codes[0][:].bitcast(FP8X4),
-                rhs_scale=w1_scales[0][:],
-                start=True,
-                stop=True,
-            )
-        round_w1_row_pair(0, 0, PACK)
-        for n in range(2):
-            gelu(0, n)
+        round_w1_row_pair(on_vector, 0, 0, PACK)
+        gelu(0, 0)
 
+        round_w1_row_pair(on_vector, 1, 0, 2)
+        round_w1_row_pair(on_vector, 1, 2, PACK, 0, P // 4)
+        round_w1_row_pair(on_scalar, 1, 2, PACK, P // 4, P // 2)
+        gelu(0, 1)
         for i in range(2):
-            round_w1_row_pair(1, 2 * i, 2 * i + 2)
-        for i in range(2):
-            columns = slice(2 * P * i, 2 * P * i + 2 * P)
-            values = slice(2 * PASS * i, 2 * PASS * i + 2 * PASS)
-            quantise(w1_codes[1][:, columns], w1_scales[1][:, columns], w1_bf[1][:, values])
+            quantise_w1(1, i)
         for n in range(2):
             first_layer(1, n)
 

@@ -15,7 +15,7 @@ K, T, H, N, V, L = 512, 1024, 1024, 256, 256, 4
 PACK = 4
 PASS = P * PACK
 W2_VECTOR_COLUMNS = 192
-WARM_ROWS = 64
+WARM_ROWS = 32
 FLOPS = 2 * V * (K * H + H * N)
 
 

@@ -132,8 +132,8 @@ def tile_picked_grid_mlp_gelu_sub_l_kernel(tc, xT, w1, w2, offs, out):
         def gelu(g, n):
             nc.scalar.activation(h_bf[g][n], h_ps[g][n][:].rearrange("p t v -> p v t"), GELU)
 
-        def second_layer(g, n, h_codes):
-            for r in range(2):
+        def second_layer(g, n, h_codes, rows=(0, 1)):
+            for r in rows:
                 nc.tensor.matmul_mx(
                     out=out_ps[r][n][:, 0:P],
                     lhsT=w2_codes[g][:, half(r)].bitcast(FP8X4),
@@ -195,10 +195,11 @@ def tile_picked_grid_mlp_gelu_sub_l_kernel(tc, xT, w1, w2, offs, out):
         h_last_codes = in_last_load_slot([P, P], U32, "h_last_codes")
         quantise(h_last_codes[:], h_last_scales[:], flat(h_last_bf[:]))
         second_layer(1, 0, tail_codes[:, half(0)])
-        second_layer(1, 1, h_last_codes[:])
+        second_layer(1, 1, h_last_codes[:], rows=(1, 0))
 
         for n in range(2):
-            nc.scalar.copy(out_sb[0][n][:], out_ps[0][n][:, 0:P])
-            (nc.scalar if n == 1 else nc.sync).dma_start(out[half(0), half(n)], out_sb[0][n][:])
-            nc.vector.tensor_copy(out_sb[1][n][:], out_ps[1][n][:, 0:P])
-            nc.sync.dma_start(out[half(1), half(n)], out_sb[1][n][:])
+            first, second = n, 1 - n
+            nc.scalar.copy(out_sb[first][n][:], out_ps[first][n][:, 0:P])
+            (nc.scalar if n == 1 else nc.sync).dma_start(out[half(first), half(n)], out_sb[first][n][:])
+            nc.vector.tensor_copy(out_sb[second][n][:], out_ps[second][n][:, 0:P])
+            nc.sync.dma_start(out[half(second), half(n)], out_sb[second][n][:])

@@ -28,16 +28,19 @@ def tile_picked_grid_mlp_gelu_sub_l_kernel(tc, xT, w1, w2, offs, out):
         def sb(shape, dtype, name):
             return held.tile(shape, dtype, name=name, align_bytes=64)
 
-        def in_last_load_slot(shape, dtype, name):
-            return held.tile(shape, dtype, name=name, tag="last_load", align_bytes=64)
+        def for_dma(shape, name):
+            return held.tile(shape, F32, name=name, align_bytes=256)
 
-        offsets = held.tile([P, L * V // 16], U16, name="offsets")
-        w1_first_raw = sb([P, PACK, PASS], F32, "w1_first_raw")
-        shared = sb([P, V + 2 * PASS], F32, "shared")
+        def in_last_load_slot(shape, dtype, name):
+            return held.tile(shape, dtype, name=name, tag="last_load", align_bytes=256)
+
+        offsets = held.tile([P, L * V // 16], U16, name="offsets", align_bytes=256)
+        w1_first_raw = for_dma([P, PACK, PASS], "w1_first_raw")
+        shared = for_dma([P, V + 2 * PASS], "shared")
         h_first_bf = shared[:, 0 : 2 * V].bitcast(BF16).rearrange("p (v j) -> p v j", j=PACK)
-        w1_pair_raw = [sb([P, 2, PASS], F32, "w1_first_pair_raw")[:], shared[:, V:].rearrange("p (j c) -> p j c", j=2)]
-        x_raw = [sb([P, T], F32, "x_raw%d" % l) for l in range(L)]
-        w2_raw = [sb([P, PACK, N], F32, "w2_first_raw"), in_last_load_slot([P, PACK, N], F32, "w2_last_raw")]
+        w1_pair_raw = [for_dma([P, 2, PASS], "w1_first_pair_raw")[:], shared[:, V:].rearrange("p (j c) -> p j c", j=2)]
+        x_raw = [for_dma([P, T], "x_raw%d" % l) for l in range(L)]
+        w2_raw = [for_dma([P, PACK, N], "w2_first_raw"), in_last_load_slot([P, PACK, N], F32, "w2_last_raw")]
 
         x_bf = sb([P, V, PACK], BF16, "x_bf")
         x_codes = [sb([P, P], U32, "x_codes%d" % n) for n in range(2)]
@@ -55,7 +58,7 @@ def tile_picked_grid_mlp_gelu_sub_l_kernel(tc, xT, w1, w2, offs, out):
         tail_scales = sb([P, P + N], U8, "tail_scales")
         h_last_bf = sb([P, P, PACK], BF16, "h_last_bf")
         h_last_scales = sb([P, P], U8, "h_last_scales")
-        out_sb = [[sb([P, P], F32, "out_sb%d%d" % (r, n)) for n in range(2)] for r in range(2)]
+        out_sb = [[for_dma([P, P], "out_sb%d%d" % (r, n)) for n in range(2)] for r in range(2)]
 
         h_ps = [[psum.tile([P, PACK, P], F32, name="h_ps%d%d" % (g, n)) for n in range(2)] for g in range(2)]
         out_ps = [[psum.tile([P, PASS], F32, name="out_ps%d%d" % (r, n)) for n in range(2)] for r in range(2)]

@@ -14,7 +14,7 @@ P = 128
 K, T, H, N, V, L = 512, 1024, 1024, 256, 256, 4
 PACK = 4
 PASS = P * PACK
-W2_VECTOR_COLUMNS = 192
+W2_VECTOR_COLUMNS = 160
 WARM_ROWS = 32
 FLOPS = 2 * V * (K * H + H * N)
 

from contextlib import ExitStack

import concourse.mybir as mybir

F32 = mybir.dt.float32
BF16 = mybir.dt.bfloat16
U32 = mybir.dt.uint32
U16 = mybir.dt.uint16
U8 = mybir.dt.uint8
FP8X4 = mybir.dt.float8_e4m3fn_x4
GELU = mybir.ActivationFunctionType.Gelu_apprx_tanh

P = 128
K, T, H, N, V, L = 512, 1024, 1024, 256, 256, 4
PACK = 4
PASS = P * PACK
W2_VECTOR_COLUMNS = 160
WARM_ROWS = 32
FLOPS = 2 * V * (K * H + H * N)


def tile_picked_grid_mlp_gelu_sub_l_kernel(tc, xT, w1, w2, offs, out):
    nc = tc.nc
    with ExitStack() as ctx:
        held = ctx.enter_context(tc.tile_pool(name="held", bufs=1))
        psum = ctx.enter_context(tc.psum_pool(name="psum", bufs=1))

        def sb(shape, dtype, name):
            return held.tile(shape, dtype, name=name, align_bytes=64)

        def for_dma(shape, name):
            return held.tile(shape, F32, name=name, align_bytes=256)

        def in_last_load_slot(shape, dtype, name):
            return held.tile(shape, dtype, name=name, tag="last_load", align_bytes=256)

        offsets = held.tile([P, L * V // 16], U16, name="offsets", align_bytes=256)
        w1_first_raw = for_dma([P, PACK, PASS], "w1_first_raw")
        shared = for_dma([P, V + 2 * PASS], "shared")
        h_first_bf = shared[:, 0 : 2 * V].bitcast(BF16).rearrange("p (v j) -> p v j", j=PACK)
        w1_pair_raw = [for_dma([P, 2, PASS], "w1_first_pair_raw")[:], shared[:, V:].rearrange("p (j c) -> p j c", j=2)]
        x_raw = [for_dma([P, T], "x_raw%d" % l) for l in range(L)]
        w2_raw = [for_dma([P, PACK, N], "w2_first_raw"), in_last_load_slot([P, PACK, N], F32, "w2_last_raw")]

        x_bf = sb([P, V, PACK], BF16, "x_bf")
        x_codes = [sb([P, P], U32, "x_codes%d" % n) for n in range(2)]
        x_scales = [sb([P, P], U8, "x_scales%d" % n) for n in range(2)]
        w1_bf = [sb([P, PASS * PACK], BF16, "w1_bf%d" % g) for g in range(2)]
        w1_codes = [sb([P, PASS], U32, "w1_codes%d" % g) for g in range(2)]
        w1_scales = [sb([P, PASS], U8, "w1_scales%d" % g) for g in range(2)]
        w2_first_bf = sb([P, N, PACK], BF16, "w2_first_bf")
        w2_first_codes = sb([P, N], U32, "w2_first_codes")
        w2_first_scales = sb([P, N], U8, "w2_first_scales")
        h_first_codes = sb([P, V], U32, "h_first_codes")
        h_first_scales = sb([P, V], U8, "h_first_scales")
        tail_bf = sb([P, P + N, PACK], BF16, "tail_bf")
        tail_codes = sb([P, P + N], U32, "tail_codes")
        tail_scales = sb([P, P + N], U8, "tail_scales")
        h_last_bf = sb([P, P, PACK], BF16, "h_last_bf")
        h_last_scales = sb([P, P], U8, "h_last_scales")
        out_sb = [[for_dma([P, P], "out_sb%d%d" % (r, n)) for n in range(2)] for r in range(2)]

        h_ps = [[psum.tile([P, PACK, P], F32, name="h_ps%d%d" % (g, n)) for n in range(2)] for g in range(2)]
        out_ps = [[psum.tile([P, PASS], F32, name="out_ps%d%d" % (r, n)) for n in range(2)] for r in range(2)]

        def half(i):
            return slice(P * i, P * i + P)

        w2_bf = [w2_first_bf[:], tail_bf[:, P:, :]]
        w2_codes = [w2_first_codes[:], tail_codes[:, P:]]
        w2_scales = [w2_first_scales[:], tail_scales[:, P:]]
        h_bf = [[h_first_bf[:, half(n), :] for n in range(2)], [tail_bf[:, half(0), :], h_last_bf[:]]]
        h_scales = [[h_first_scales[:, half(n)] for n in range(2)], [tail_scales[:, half(0)], h_last_scales[:]]]

        w1_rows = w1.rearrange("(p j) c -> p j c", j=PACK)
        w2_rows = w2.rearrange("(g p j) c -> g p j c", g=2, j=PACK)
        x_rows = xT.rearrange("(p l) c -> p l c", l=L)
        nc.sync.dma_start(offsets[:], offs)
        nc.sync.dma_start(w1_first_raw[:], w1_rows[:, :, 0:PASS])
        nc.scalar.dma_start(x_raw[0][:], x_rows[:, 0, :])
        for l in range(1, L):
            nc.sync.dma_start(x_raw[l][:], x_rows[:, l, :])
        for pair in range(2):
            nc.sync.dma_start(w1_pair_raw[pair], w1_rows[:, 2 * pair : 2 * pair + 2, PASS:H])
        for g in range(2):
            nc.sync.dma_start(w2_raw[g][:], w2_rows[g])

        def round_w1_first_half(copy, t0, t1):
            copy(
                w1_bf[0][:].rearrange("p (t m j) -> p m t j", t=PACK, j=PACK)[:, :, t0:t1],
                w1_first_raw[:].rearrange("p j (m t) -> p m t j", t=PACK)[:, :, t0:t1],
            )

        def round_w1_row_pair(copy, pair, t0, t1, q0=0, q1=P // 2):
            slots = slice(2 * pair, 2 * pair + 2)
            copy(
                w1_bf[1][:].rearrange("p (t q e j) -> p q t e j", t=PACK, e=2, j=PACK)[:, q0:q1, t0:t1, :, slots],
                w1_pair_raw[pair].rearrange("p j (q e t) -> p q t e j", e=2, t=PACK)[:, q0:q1, t0:t1],
            )

        def round_w2(copy, g, lo, hi):
            copy(
                w2_bf[g][:, lo:hi, :].rearrange("p (c e) j -> p c j e", e=4),
                w2_raw[g][:, :, lo:hi].rearrange("p j (c e) -> p c j e", e=4),
            )

        def flat(ap):
            return ap.rearrange("p c j -> p (c j)")

        def quantise(codes, scales, rounded):
            nc.vector.quantize_mx(out=codes.bitcast(FP8X4), scales=scales, in_=rounded)

        def quantise_w1(g, i):
            columns = slice(2 * P * i, 2 * P * i + 2 * P)
            values = slice(2 * PASS * i, 2 * PASS * i + 2 * PASS)
            quantise(w1_codes[g][:, columns], w1_scales[g][:, columns], w1_bf[g][:, values])

        def look_up(l, lo, hi):
            first = l * V + lo
            entries = offsets[:, first // 16 : (first + hi - lo) // 16]
            nc.vector.tensor_copy(x_bf[:, lo:hi, l], x_raw[l][:].indirect(entries))

        def first_layer(g, n):
            for t in range(PACK):
                nc.tensor.matmul_mx(
                    out=h_ps[g][n][:, t, :],
                    lhsT=w1_codes[g][:, half(t)].bitcast(FP8X4),
                    lhsT_scale=w1_scales[g][:, half(t)],
                    rhs=x_codes[n][:].bitcast(FP8X4),
                    rhs_scale=x_scales[n][:],
                    start=True,
                    stop=True,
                )

        def gelu(g, n):
            nc.scalar.activation(h_bf[g][n], h_ps[g][n][:].rearrange("p t v -> p v t"), GELU)

        def second_layer(g, n, h_codes, rows=(0, 1)):
            for r in rows:
                nc.tensor.matmul_mx(
                    out=out_ps[r][n][:, 0:P],
                    lhsT=w2_codes[g][:, half(r)].bitcast(FP8X4),
                    lhsT_scale=w2_scales[g][:, half(r)],
                    rhs=h_codes.bitcast(FP8X4),
                    rhs_scale=h_scales[g][n],
                    start=(g == 0),
                    stop=(g == 1),
                )

        on_vector, on_scalar = nc.vector.tensor_copy, nc.scalar.copy

        round_w1_first_half(on_vector, 0, 2)
        round_w1_first_half(on_scalar, 2, PACK)
        for i in range(2):
            quantise_w1(0, i)
        for r in range(2):
            nc.tensor.matmul_mx(
                out=out_ps[r][1][0:WARM_ROWS, :],
                lhsT=w1_codes[0][:, 0:WARM_ROWS].bitcast(FP8X4),
                lhsT_scale=w1_scales[0][:, 0:WARM_ROWS],
                rhs=w1_codes[0][:].bitcast(FP8X4),
                rhs_scale=w1_scales[0][:],
                start=True,
                stop=True,
            )
        for l in range(L - 1):
            look_up(l, 0, V)
        for n in range(2):
            look_up(L - 1, P * n, P * n + P)
            quantise(x_codes[n][:], x_scales[n][:], flat(x_bf[:, half(n), :]))
        for n in range(2):
            first_layer(0, n)
        round_w1_row_pair(on_vector, 0, 0, PACK)
        gelu(0, 0)

        round_w1_row_pair(on_vector, 1, 0, 2)
        round_w1_row_pair(on_vector, 1, 2, PACK, 0, P // 4)
        round_w1_row_pair(on_scalar, 1, 2, PACK, P // 4, P // 2)
        gelu(0, 1)
        for i in range(2):
            quantise_w1(1, i)
        for n in range(2):
            first_layer(1, n)

        round_w2(on_scalar, 0, W2_VECTOR_COLUMNS, N)
        round_w2(on_vector, 0, 0, W2_VECTOR_COLUMNS)
        quantise(w2_codes[0], w2_scales[0], flat(w2_bf[0]))
        for n in range(2):
            gelu(1, n)
        quantise(h_first_codes[:], h_first_scales[:], flat(h_first_bf))
        for n in range(2):
            second_layer(0, n, h_first_codes[:, half(n)])

        for r in range(2):
            round_w2(on_vector, 1, P * r, P * r + P)
        for columns in (slice(0, 2 * P), slice(2 * P, P + N)):
            quantise(tail_codes[:, columns], tail_scales[:, columns], flat(tail_bf[:, columns, :]))
        h_last_codes = in_last_load_slot([P, P], U32, "h_last_codes")
        quantise(h_last_codes[:], h_last_scales[:], flat(h_last_bf[:]))
        second_layer(1, 0, tail_codes[:, half(0)])
        second_layer(1, 1, h_last_codes[:], rows=(1, 0))

        for n in range(2):
            first, second = n, 1 - n
            nc.scalar.copy(out_sb[first][n][:], out_ps[first][n][:, 0:P])
            (nc.scalar if n == 1 else nc.sync).dma_start(out[half(first), half(n)], out_sb[first][n][:])
            nc.vector.tensor_copy(out_sb[second][n][:], out_ps[second][n][:, 0:P])
            nc.sync.dma_start(out[half(second), half(n)], out_sb[second][n][:])
